import numpy as np
import ml_dtypes


def mxq(x, axis, fmt="e4m3"):
    dtype, down = {"e4m3": (ml_dtypes.float8_e4m3fn, 7), "e5m2": (ml_dtypes.float8_e5m2, 14)}[fmt]
    v = np.moveaxis(np.asarray(x, np.float32).astype(ml_dtypes.bfloat16).astype(np.float64), axis, -1)
    blocks = v.reshape(v.shape[:-1] + (-1, 32))
    amax = np.abs(blocks).max(-1, keepdims=True)
    byte = np.maximum(np.where(amax > 0, np.frexp(amax)[1] - 1 + 127, 0) - down, 1)
    scale = np.exp2(byte - 127.0)
    codes = (blocks / scale).astype(np.float32).astype(dtype).astype(np.float64)
    return np.moveaxis((codes * scale).reshape(v.shape), -1, axis)


WIDE = False


def mx_kscale(k):
    if not WIDE:
        return np.ones(k)
    levels = np.array([10, -10, 5, -5, 0])
    if k % 512:
        return np.exp2(np.random.permutation(np.resize(levels, k // 32))).repeat(32)
    a = np.empty((k // 512, 16))
    for p in range(k // 512):
        a[p, :8] = np.random.permutation(np.resize(levels, 8))
        for g in range(8):
            far = levels[np.abs(levels - a[p, g]) >= 10]
            a[p, g + 8] = far[np.random.randint(len(far))]
    return np.exp2(a.ravel()).repeat(32)


def f64(x):
    return np.asarray(x).astype(np.float64)


def striped(idx):
    return np.tile(idx.reshape(-1, 16).T, (8, 1)).astype(np.uint16)


def unstriped(offs):
    return offs[:16].T.reshape(-1).astype(np.int64)


def striped8(idx):
    return np.concatenate([x.reshape(-1, 16).T for x in idx]).astype(np.uint16)


def runs(offs, k):
    lists = np.stack([offs[16 * r : 16 * r + 16].T.reshape(-1) for r in range(8)]).astype(np.int64)
    return lists[np.arange(k) % 512 // 64]


def pack_weight(w):
    k, n = w.shape
    w = f64(np.asarray(w, np.float32).astype(ml_dtypes.bfloat16)).reshape(k // 32, 32, n)
    amax = np.abs(w).max(1)
    byte = np.clip(np.where(amax > 0, np.frexp(amax)[1] - 1 + 127 - 7, 1), 1, 254)
    scaled = (w * np.exp2(127.0 - byte)[:, None, :]).reshape(k, n).astype(np.float32)
    words = np.ascontiguousarray(scaled.reshape(k // 512, 128, 4, n).transpose(0, 1, 3, 2)).astype(ml_dtypes.float8_e4m3fn).view(np.uint8)
    return words, np.ascontiguousarray(byte.astype(np.uint8).reshape(k // 512, 16, n))


def unpack_weight(words, scales):
    g, p, n, _ = words.shape
    vals = np.ascontiguousarray(words).view(ml_dtypes.float8_e4m3fn).astype(np.float64) * np.repeat(np.exp2(scales.astype(np.float64) - 127.0), 8, axis=1)[..., None]
    return vals.transpose(0, 1, 3, 2).reshape(g * 512, n)


E2M1 = np.array([0.0, 0.5, 1.0, 1.5, 2.0, 3.0, 4.0, 6.0, -0.0, -0.5, -1.0, -1.5, -2.0, -3.0, -4.0, -6.0])


def pack_fp4(w):
    k, n = w.shape
    w = f64(np.asarray(w, np.float32).astype(ml_dtypes.bfloat16)).reshape(k // 32, 32, n)
    amax = np.abs(w).max(1)
    mant, ex = np.frexp(amax / 6.0)
    byte = np.clip(np.where(amax > 0, np.where(mant > 0.5, ex, ex - 1) + 127, 1), 1, 254)
    scaled = (w * np.exp2(127.0 - byte)[:, None, :]).reshape(k, n).astype(np.float32)
    c = np.ascontiguousarray(scaled.reshape(k // 512, 128, 4, n).transpose(0, 1, 3, 2)).astype(ml_dtypes.float4_e2m1fn).view(np.uint8) & 0xF
    words = (c[..., 0::2] | (c[..., 1::2] << 4)).reshape(k // 512, 128, 2 * n)
    return np.ascontiguousarray(words), np.ascontiguousarray(byte.astype(np.uint8).reshape(k // 512, 16, n))


def unpack_fp4(words, scales):
    g, _, n = scales.shape
    words = np.ascontiguousarray(words).reshape(g, 128, n, 2)
    nib = np.empty((g, 128, n, 4), np.uint8)
    nib[..., 0::2] = words & 0xF
    nib[..., 1::2] = words >> 4
    vals = E2M1[nib] * np.repeat(np.exp2(scales.astype(np.float64) - 127.0), 8, axis=1)[..., None]
    return vals.transpose(0, 1, 3, 2).reshape(g * 512, n)


def planes(y):
    n, m = y.shape
    v = y.astype(np.float32).astype(ml_dtypes.bfloat16).astype(np.float64).reshape(n // 32, 32, m)
    top = np.abs(v).max(1)
    byte = np.clip(np.where(top > 0, np.frexp(top)[1] - 1 + 127 - 7, 1), 1, 254)
    codes = (v * np.exp2(127.0 - byte)[:, None, :]).reshape(n, m).astype(np.float32).astype(ml_dtypes.float8_e4m3fn).view(np.uint8)
    words = codes.reshape(n // 512, 128, 4, m).transpose(0, 1, 3, 2)
    return np.ascontiguousarray(words), np.ascontiguousarray(byte.astype(np.uint8).reshape(n // 512, 16, m))


K, T, S, H, W, C = 512, 2048, 512, 512, 2048, 512


def setup_inputs():
    n = np.random.standard_normal
    s = mx_kscale(K)[:, None]
    packed_xT = pack_weight(n((K, T)) * s)
    packed_w1 = pack_fp4(n((K, H)) / np.sqrt(K) / s)
    return {
        "x_words": packed_xT[0],
        "x_scales": packed_xT[1],
        "w1_words": packed_w1[0],
        "w1_scales": packed_w1[1],
        "gs": (np.random.uniform(0.5, 1.5, (K, 1)) / s).astype(np.float32),
        "gs2": (np.random.uniform(0.5, 1.5, (K, 1)) / s).astype(np.float32),
        "offs": striped(np.random.permutation(T)[:S]),
        "n1": striped8(np.stack([np.random.permutation(S) for _ in range(8)])),
        "n2": striped8(np.stack([np.random.permutation(S) for _ in range(8)])),
        "n3": striped(np.random.randint(0, S, W)),
        "ca": striped(np.random.permutation(T)[:C]),
        "cb": striped(np.random.permutation(T)[:C]),
        "n4": striped(np.random.permutation(S)),
        "n5": striped(np.random.permutation(S)),
    }


def reference(x_words, x_scales, w1_words, w1_scales, gs, gs2, offs, n1, n2, n3, ca, cb, n4, n5):
    x_ca = unpack_weight(x_words, x_scales)[:, unstriped(ca)]
    xq = unpack_weight(x_words, x_scales)[:, unstriped(offs)]
    y = unpack_fp4(w1_words, w1_scales).T @ xq
    pa = y[np.arange(H)[:, None], runs(n1, H)]
    pb = y[np.arange(H)[:, None], runs(n2, H)]
    z = f64(gs) * (np.maximum(np.minimum(y, pa), np.minimum(np.maximum(y, pa), pb)))
    a = 0.0625 * ((x_ca.T @ mxq(z, 0, "e4m3")))
    x_cb = unpack_weight(x_words, x_scales)[:, unstriped(cb)]
    mb = y[:, unstriped(n3)]
    mx = mb.reshape(H, S, 4).max(axis=2)
    mn = mb.reshape(H, S, 4).min(axis=2)
    z2 = f64(gs2) * (mx * np.tanh(y - mn))
    b = 0.0625 * ((x_cb.T @ mxq(z2, 0, "e4m3")))
    out_0 = np.maximum(a, b[:, unstriped(n5)]) - (np.minimum(a[:, unstriped(n4)], b))
    return (out_0,) + planes(out_0)

@@ -1,0 +1,255 @@
+from contextlib import ExitStack
+
+import concourse.mybir as mybir
+
+F32 = mybir.dt.float32
+BF16 = mybir.dt.bfloat16
+I32 = mybir.dt.int32
+U32 = mybir.dt.uint32
+U16 = mybir.dt.uint16
+U8 = mybir.dt.uint8
+FP8X4 = mybir.dt.float8_e4m3fn_x4
+FP4X4 = mybir.dt.float4_e2m1fn_x4
+ALU = mybir.AluOpType
+ACT = mybir.ActivationFunctionType
+
+P = 128
+PACK = 4
+K, T, S = 512, 2048, 512
+MEMBERS = 4
+HALF = S // 2
+HALVES = (slice(0, HALF), slice(HALF, S))
+LAG = 3
+SPARE = 16
+SCORE_SCALE = 0.0625
+FLOPS = 3 * 2 * K * S * S
+
+
+def tile_picked_twocdmaxbmedgtan_none_po_kernel(
+    tc, x_words, x_scales, w1_words, w1_scales, gs, gs2, offs, n1, n2, n3, ca, cb, n4, n5, out_0, out_1, out_2
+):
+    nc = tc.nc
+    with ExitStack() as ctx:
+        held = ctx.enter_context(tc.tile_pool(name="held", bufs=1))
+        ring = ctx.enter_context(tc.tile_pool(name="ring", bufs=3))
+        late = ctx.enter_context(tc.tile_pool(name="late", bufs=LAG + 2))
+        psum = ctx.enter_context(tc.psum_pool(name="psum", bufs=1))
+
+        def load_list(src, name):
+            lst = held.tile([P, src.shape[1]], U16, name=name)
+            nc.sync.dma_start(lst[:], src)
+            return lst
+
+        def entries(lst, first, count):
+            return lst[:, first // 16 : (first + count) // 16]
+
+        def load_scale_rows(queue, plane, src, quadrant):
+            queue.dma_start(
+                plane[32 * quadrant : 32 * quadrant + 4, :].bitcast(I32),
+                src[0, 4 * quadrant : 4 * quadrant + 4, :].bitcast(I32),
+            )
+
+        xw = held.tile([P, T], U32, name="xw")
+        xs = held.tile([P, T], U8, name="xs")
+        ww = held.tile([P, 2 * S], U8, name="ww")
+        ws = held.tile([P, S], U8, name="ws")
+        nc.vector.memset(xs[:].bitcast(I32), 0)
+        nc.vector.memset(ws[:].bitcast(I32), 0)
+        offs_l = load_list(offs, "offs_l")
+        nc.sync.dma_start(ww[:], w1_words[0])
+        n3_l = load_list(n3, "n3_l")
+        nc.sync.dma_start(xw[:].bitcast(I32), x_words[0].rearrange("p c r -> p (c r)").bitcast(I32))
+        for q in range(4):
+            load_scale_rows(nc.sync, xs, x_scales, q)
+        for q in range(4):
+            load_scale_rows(nc.sync if q < 3 else nc.gpsimd, ws, w1_scales, q)
+        g1 = held.tile([P, PACK], F32, name="g1")
+        g2 = held.tile([P, PACK], F32, name="g2")
+        cb_l = load_list(cb, "cb_l")
+        nc.sync.dma_start(g1[:], gs.rearrange("(p t) o -> p (t o)", t=PACK))
+        ca_l = load_list(ca, "ca_l")
+        n1_l = load_list(n1, "n1_l")
+        n2_l = load_list(n2, "n2_l")
+        nc.sync.dma_start(g2[:], gs2.rearrange("(p t) o -> p (t o)", t=PACK))
+        n5_l = load_list(n5, "n5_l")
+        n4_l = load_list(n4, "n4_l")
+
+        y = [held.tile([P, S + SPARE], F32, name=f"y{t}") for t in range(PACK)]
+        for t in range(PACK):
+            nc.vector.memset(y[t][:, S:], 0.0)
+
+        wwd = held.tile([P, PACK, P, 2], U8, name="wwd", align_bytes=64)
+        wsd = held.tile([P, PACK, P], U8, name="wsd", align_bytes=64)
+        nc.vector.tensor_copy(wwd[:], ww[:].rearrange("p (m t b) -> p t m b", t=PACK, b=2))
+        nc.vector.tensor_copy(wsd[:], ws[:].rearrange("p (m t) -> p t m", t=PACK))
+
+        def pick(lst, name):
+            words = held.tile([P, S], U32, name=f"{name}_words", align_bytes=64)
+            scales = held.tile([P, S], U8, name=f"{name}_scales", align_bytes=64)
+            nc.vector.tensor_copy(words[:], xw[:].indirect(lst[:]))
+            nc.vector.tensor_copy(scales[:], xs[:].indirect(lst[:]))
+            return words, scales
+
+        def pick_dealt(lst, name):
+            words, scales = pick(lst, name)
+            dealt_words = held.tile([P, PACK, P], U32, name=f"{name}_dealt_words", align_bytes=64)
+            dealt_scales = held.tile([P, PACK, P], U8, name=f"{name}_dealt_scales", align_bytes=64)
+            nc.vector.tensor_copy(
+                dealt_words[:].bitcast(I32), words[:].bitcast(I32).rearrange("p (m t) -> p t m", t=PACK)
+            )
+            nc.vector.tensor_copy(dealt_scales[:], scales[:].rearrange("p (m t) -> p t m", t=PACK))
+            return dealt_words, dealt_scales
+
+        xq_words, xq_scales = pick(offs_l, "xq")
+        for t in range(PACK):
+            bank = psum.tile([P, S], F32, name=f"bank_y{t}", tag=f"first{t}")
+            nc.tensor.matmul_mx(
+                out=bank[:],
+                lhsT=wwd[:, t].rearrange("p m b -> p (m b)").bitcast(FP4X4),
+                lhsT_scale=wsd[:, t],
+                rhs=xq_words[:].bitcast(FP8X4),
+                rhs_scale=xq_scales[:],
+                start=True,
+                stop=True,
+            )
+            nc.scalar.activation(y[t][:, :S], bank[:], ACT.Copy)
+
+        xb_words, xb_scales = pick_dealt(cb_l, "xb")
+        yg = [held.tile([P, S], F32, name=f"yg{t}") for t in range(PACK)]
+        for t in range(PACK):
+            nc.vector.tensor_scalar(yg[t][:], y[t][:, :S], g1[:, t : t + 1], None, ALU.mult)
+        xa_words, xa_scales = pick_dealt(ca_l, "xa")
+
+        def by_fours(ap, order):
+            return ap.rearrange(order + " -> p c t i", i=4)
+
+        def score(grouped, name, words, scales, banks, cols):
+            codes = held.tile([P, cols.stop - cols.start], U32, name=f"{name}_codes", align_bytes=64)
+            plane = held.tile([P, cols.stop - cols.start], U8, name=f"{name}_plane", align_bytes=64)
+            nc.vector.quantize_mx(
+                out=codes[:].bitcast(FP8X4), scales=plane[:], in_=grouped[:].rearrange("p c t -> p (c t)")
+            )
+            for t in range(PACK):
+                nc.tensor.matmul_mx(
+                    out=banks[t][:, cols],
+                    lhsT=words[:, t].bitcast(FP8X4),
+                    lhsT_scale=scales[:, t],
+                    rhs=codes[:].bitcast(FP8X4),
+                    rhs_scale=plane[:],
+                    start=True,
+                    stop=True,
+                )
+
+        b_banks = [psum.tile([P, S], F32, name=f"bank_b{t}", tag=f"first{t}") for t in range(PACK)]
+        z2 = held.tile([P, PACK, S], F32, name="z2")
+
+        def extremes(t, cols):
+            mb = ring.tile([P, HALF, MEMBERS], F32, name="mb", tag="picked")
+            for c in range(2):
+                nc.scalar.activation(
+                    mb[:, c * HALF // 2 : (c + 1) * HALF // 2, :].rearrange("p j m -> p (j m)"),
+                    y[t][:].indirect(entries(n3_l, MEMBERS * (cols.start + c * HALF // 2), MEMBERS * HALF // 2)),
+                    ACT.Copy,
+                )
+            lo = ring.tile([P, HALF, 2], F32, name="lo")
+            hi = ring.tile([P, HALF, 2], F32, name="hi")
+            mn = ring.tile([P, HALF], F32, name="mn")
+            mx = late.tile([P, HALF], F32, name="mx")
+            gap = late.tile([P, HALF], F32, name="gap")
+            th = late.tile([P, HALF], F32, name="th")
+            nc.vector.tensor_tensor(lo[:], mb[:, :, 0:2], mb[:, :, 2:4], ALU.min)
+            nc.vector.tensor_tensor(hi[:], mb[:, :, 0:2], mb[:, :, 2:4], ALU.max)
+            nc.vector.tensor_tensor(mn[:], lo[:, :, 0], lo[:, :, 1], ALU.min)
+            nc.vector.tensor_tensor(mx[:], hi[:, :, 0], hi[:, :, 1], ALU.max)
+            nc.vector.tensor_tensor(gap[:], y[t][:, cols], mn[:], ALU.subtract)
+            nc.scalar.activation(th[:], gap[:], ACT.Tanh)
+            return lambda: nc.vector.scalar_tensor_tensor(
+                z2[:, t, cols], mx[:], g2[:, t : t + 1], th[:], ALU.mult, ALU.mult
+            )
+
+        low = held.tile([P, PACK, S], F32, name="low")
+        cut = held.tile([P, PACK, S], F32, name="cut")
+
+        pab0 = held.tile([P, 2, S], F32, name="pab0")
+
+        def neighbours(t, which, cols):
+            return yg[t][:].indirect(entries((n1_l, n2_l)[which], cols.start, HALF))
+
+        def median_parts(t):
+            high = ring.tile([P, S], F32, name="high")
+            if t == 0:
+                pab = pab0
+            else:
+                pab = ring.tile([P, 2, S], F32, name="pab", tag="picked")
+                for which in range(2):
+                    for cols in HALVES:
+                        nc.scalar.activation(pab[:, which, cols], neighbours(t, which, cols), ACT.Copy)
+            nc.vector.tensor_tensor(high[:], yg[t][:], pab[:, 0, :], ALU.max)
+            nc.vector.tensor_tensor(low[:, t, :], yg[t][:], pab[:, 0, :], ALU.min)
+            nc.vector.tensor_tensor(cut[:, t, :], high[:], pab[:, 1, :], ALU.min)
+
+        waiting = []
+        for t in range(PACK):
+            for cols in HALVES:
+                waiting.append(extremes(t, cols))
+                if len(waiting) > LAG:
+                    waiting.pop(0)()
+            nc.vector.tensor_copy(pab0[:, t // 2, HALVES[t % 2]], neighbours(0, t // 2, HALVES[t % 2]))
+        median_parts(0)
+        for finish in waiting:
+            finish()
+        z2_grouped = held.tile([P, S, PACK], BF16, name="z2_grouped", align_bytes=64)
+        nc.vector.tensor_copy(by_fours(z2_grouped[:], "p (c i) t"), by_fours(z2[:], "p t (c i)"))
+        score(z2_grouped, "z2", xb_words, xb_scales, b_banks, slice(0, S))
+        for t in range(1, PACK):
+            median_parts(t)
+
+        b = [held.tile([P, S], F32, name=f"b{t}") for t in range(PACK)]
+        bn = [held.tile([P, S], F32, name=f"bn{t}") for t in range(PACK)]
+        for t in range(PACK):
+            nc.scalar.activation(b[t][:], b_banks[t][:], ACT.Copy, scale=SCORE_SCALE)
+            for cols in HALVES:
+                nc.scalar.activation(bn[t][:, cols], b[t][:].indirect(entries(n5_l, cols.start, HALF)), ACT.Copy)
+
+        a_banks = [psum.tile([P, S], F32, name=f"bank_a{t}", tag=f"second{t}") for t in range(PACK)]
+        a = [held.tile([P, S], F32, name=f"a{t}") for t in range(PACK)]
+        z_grouped = [held.tile([P, HALF, PACK], BF16, name=f"z_grouped{h}", align_bytes=64) for h in range(2)]
+        for h, cols in enumerate(HALVES):
+            nc.vector.tensor_tensor(
+                by_fours(z_grouped[h][:], "p (c i) t"),
+                by_fours(low[:, :, cols], "p t (c i)"),
+                by_fours(cut[:, :, cols], "p t (c i)"),
+                ALU.max,
+            )
+            score(z_grouped[h], f"z_{h}", xa_words, xa_scales, a_banks, cols)
+            for t in range(PACK):
+                nc.scalar.activation(a[t][:, cols], a_banks[t][:, cols], ACT.Copy, scale=SCORE_SCALE)
+
+        out_rows = out_0.rearrange("(p t) j -> p t j", t=PACK)
+        out_words = out_1[0].rearrange("p c r -> p (c r)").bitcast(I32)
+        out_plane = held.tile([P, S], U8, name="out_plane", align_bytes=64)
+        for h in range(2):
+            cols = slice(h * HALF, (h + 1) * HALF)
+            result = held.tile([P, PACK, HALF], F32, name=f"result{h}")
+            for t in range(PACK):
+                an = ring.tile([P, HALF], F32, name="an")
+                larger = ring.tile([P, HALF], F32, name="larger")
+                smaller = ring.tile([P, HALF], F32, name="smaller")
+                nc.scalar.activation(an[:], a[t][:].indirect(entries(n4_l, h * HALF, HALF)), ACT.Copy)
+                nc.vector.tensor_tensor(larger[:], a[t][:, cols], bn[t][:, cols], ALU.max)
+                nc.vector.tensor_tensor(smaller[:], an[:], b[t][:, cols], ALU.min)
+                nc.vector.tensor_tensor(result[:, t, :], larger[:], smaller[:], ALU.subtract)
+                nc.sync.dma_start(out_rows[:, t, cols], result[:, t, :])
+            out_grouped = held.tile([P, HALF, PACK], BF16, name=f"out_grouped{h}", align_bytes=64)
+            out_codes = held.tile([P, HALF], U32, name=f"out_codes{h}", align_bytes=64)
+            nc.vector.tensor_copy(by_fours(out_grouped[:], "p (c i) t"), by_fours(result[:], "p t (c i)"))
+            nc.vector.quantize_mx(
+                out=out_codes[:].bitcast(FP8X4),
+                scales=out_plane[:, cols],
+                in_=out_grouped[:].rearrange("p c t -> p (c t)"),
+            )
+            nc.sync.dma_start(out_words[:, cols], out_codes[:].bitcast(I32))
+        for q in range(4):
+            nc.sync.dma_start(
+                out_2[0, 4 * q : 4 * q + 4, :].bitcast(I32), out_plane[32 * q : 32 * q + 4, :].bitcast(I32)
+            )

@@ -15,12 +15,18 @@ ACT = mybir.ActivationFunctionType
 
 P = 128
 PACK = 4
+QUADRANTS = 4
 K, T, S = 512, 2048, 512
 MEMBERS = 4
 HALF = S // 2
 HALVES = (slice(0, HALF), slice(HALF, S))
-LAG = 3
-SPARE = 16
+LIST_COLUMN = 16
+MEMBER_RUN = MEMBERS * HALF
+Y_WINDOW = MEMBER_RUN + LIST_COLUMN
+STEPS = PACK * len(HALVES)
+MEMBER_BUFFERS = 3
+LAG = MEMBER_BUFFERS
+VECTOR_PIECES, PA_STEP, PB_STEP = 3, 1, 4
 SCORE_SCALE = 0.0625
 FLOPS = 3 * 2 * K * S * S
 
@@ -31,225 +37,243 @@ def tile_picked_twocdmaxbmedgtan_none_po_kernel(
     nc = tc.nc
     with ExitStack() as ctx:
         held = ctx.enter_context(tc.tile_pool(name="held", bufs=1))
-        ring = ctx.enter_context(tc.tile_pool(name="ring", bufs=3))
+        ring = ctx.enter_context(tc.tile_pool(name="ring", bufs=2))
         late = ctx.enter_context(tc.tile_pool(name="late", bufs=LAG + 2))
         psum = ctx.enter_context(tc.psum_pool(name="psum", bufs=1))
 
         def load_list(src, name):
-            lst = held.tile([P, src.shape[1]], U16, name=name)
-            nc.sync.dma_start(lst[:], src)
-            return lst
+            offsets = held.tile([P, src.shape[1]], U16, name=name)
+            nc.sync.dma_start(offsets[:], src)
+            return offsets
 
-        def entries(lst, first, count):
-            return lst[:, first // 16 : (first + count) // 16]
+        def entries(offsets, first, count):
+            return offsets[:, first // LIST_COLUMN : (first + count) // LIST_COLUMN]
 
-        def load_scale_rows(queue, plane, src, quadrant):
-            queue.dma_start(
-                plane[32 * quadrant : 32 * quadrant + 4, :].bitcast(I32),
-                src[0, 4 * quadrant : 4 * quadrant + 4, :].bitcast(I32),
+        def scale_rows(tile, dram, quadrant):
+            return (
+                tile[32 * quadrant : 32 * quadrant + 4, :].bitcast(I32),
+                dram[0, 4 * quadrant : 4 * quadrant + 4, :].bitcast(I32),
             )
 
-        xw = held.tile([P, T], U32, name="xw")
-        xs = held.tile([P, T], U8, name="xs")
-        ww = held.tile([P, 2 * S], U8, name="ww")
-        ws = held.tile([P, S], U8, name="ws")
-        nc.vector.memset(xs[:].bitcast(I32), 0)
-        nc.vector.memset(ws[:].bitcast(I32), 0)
-        offs_l = load_list(offs, "offs_l")
-        nc.sync.dma_start(ww[:], w1_words[0])
-        n3_l = load_list(n3, "n3_l")
-        nc.sync.dma_start(xw[:].bitcast(I32), x_words[0].rearrange("p c r -> p (c r)").bitcast(I32))
-        for q in range(4):
-            load_scale_rows(nc.sync, xs, x_scales, q)
-        for q in range(4):
-            load_scale_rows(nc.sync if q < 3 else nc.gpsimd, ws, w1_scales, q)
-        g1 = held.tile([P, PACK], F32, name="g1")
-        g2 = held.tile([P, PACK], F32, name="g2")
-        cb_l = load_list(cb, "cb_l")
-        nc.sync.dma_start(g1[:], gs.rearrange("(p t) o -> p (t o)", t=PACK))
-        ca_l = load_list(ca, "ca_l")
-        n1_l = load_list(n1, "n1_l")
-        n2_l = load_list(n2, "n2_l")
-        nc.sync.dma_start(g2[:], gs2.rearrange("(p t) o -> p (t o)", t=PACK))
-        n5_l = load_list(n5, "n5_l")
-        n4_l = load_list(n4, "n4_l")
+        def load_weights(src, name):
+            weights = held.tile([P, PACK], F32, name=name)
+            nc.sync.dma_start(weights[:], src.rearrange("(p t) o -> p (t o)", t=PACK))
+            return weights
 
-        y = [held.tile([P, S + SPARE], F32, name=f"y{t}") for t in range(PACK)]
+        x_word_table = held.tile([P, T], U32, name="x_word_table")
+        x_scale_table = held.tile([P, T], U8, name="x_scale_table")
+        w_words = held.tile([P, 2 * S], U8, name="w_words")
+        w_scales = held.tile([P, S], U8, name="w_scales")
+        nc.vector.memset(x_scale_table[:].bitcast(I32), 0)
+        nc.vector.memset(w_scales[:].bitcast(I32), 0)
+        offs_list = load_list(offs, "offs_list")
+        n3_list = load_list(n3, "n3_list")
+        nc.sync.dma_start(w_words[:], w1_words[0])
+        for q in range(QUADRANTS):
+            nc.sync.dma_start(*scale_rows(x_scale_table, x_scales, q))
+        nc.sync.dma_start(x_word_table[:].bitcast(I32), x_words[0].rearrange("p c r -> p (c r)").bitcast(I32))
+        for q in range(QUADRANTS):
+            nc.sync.dma_start(*scale_rows(w_scales, w1_scales, q))
+        gs_rows = load_weights(gs, "gs_rows")
+        n1_list = load_list(n1, "n1_list")
+        cb_list = load_list(cb, "cb_list")
+        ca_list = load_list(ca, "ca_list")
+        n2_list = load_list(n2, "n2_list")
+        gs2_rows = load_weights(gs2, "gs2_rows")
+        n5_list = load_list(n5, "n5_list")
+        n4_list = load_list(n4, "n4_list")
+
+        y = [held.tile([P, Y_WINDOW], F32, name=f"y{t}") for t in range(PACK)]
         for t in range(PACK):
             nc.vector.memset(y[t][:, S:], 0.0)
 
-        wwd = held.tile([P, PACK, P, 2], U8, name="wwd", align_bytes=64)
-        wsd = held.tile([P, PACK, P], U8, name="wsd", align_bytes=64)
-        nc.vector.tensor_copy(wwd[:], ww[:].rearrange("p (m t b) -> p t m b", t=PACK, b=2))
-        nc.vector.tensor_copy(wsd[:], ws[:].rearrange("p (m t) -> p t m", t=PACK))
+        w_dealt_words = held.tile([P, PACK, P, 2], U8, name="w_dealt_words", align_bytes=64)
+        w_dealt_scales = held.tile([P, PACK, P], U8, name="w_dealt_scales", align_bytes=64)
+        nc.vector.tensor_copy(w_dealt_words[:], w_words[:].rearrange("p (m t b) -> p t m b", t=PACK, b=2))
+        nc.vector.tensor_copy(w_dealt_scales[:], w_scales[:].rearrange("p (m t) -> p t m", t=PACK))
 
-        def pick(lst, name):
+        def pick(offsets, name):
             words = held.tile([P, S], U32, name=f"{name}_words", align_bytes=64)
             scales = held.tile([P, S], U8, name=f"{name}_scales", align_bytes=64)
-            nc.vector.tensor_copy(words[:], xw[:].indirect(lst[:]))
-            nc.vector.tensor_copy(scales[:], xs[:].indirect(lst[:]))
+            nc.vector.tensor_copy(words[:], x_word_table[:].indirect(offsets[:]))
+            nc.vector.tensor_copy(scales[:], x_scale_table[:].indirect(offsets[:]))
             return words, scales
 
-        def pick_dealt(lst, name):
-            words, scales = pick(lst, name)
+        def pick_dealt(offsets, name):
+            words, scales = pick(offsets, name)
             dealt_words = held.tile([P, PACK, P], U32, name=f"{name}_dealt_words", align_bytes=64)
             dealt_scales = held.tile([P, PACK, P], U8, name=f"{name}_dealt_scales", align_bytes=64)
             nc.vector.tensor_copy(
-                dealt_words[:].bitcast(I32), words[:].bitcast(I32).rearrange("p (m t) -> p t m", t=PACK)
+                dealt_words[:].bitcast(I32).rearrange("p t m -> p m t"),
+                words[:].bitcast(I32).rearrange("p (m t) -> p m t", t=PACK),
             )
             nc.vector.tensor_copy(dealt_scales[:], scales[:].rearrange("p (m t) -> p t m", t=PACK))
             return dealt_words, dealt_scales
 
-        xq_words, xq_scales = pick(offs_l, "xq")
+        xq_words, xq_scales = pick(offs_list, "xq")
         for t in range(PACK):
-            bank = psum.tile([P, S], F32, name=f"bank_y{t}", tag=f"first{t}")
+            y_bank = psum.tile([P, S], F32, name=f"y_bank{t}", tag=f"y_then_b{t}")
             nc.tensor.matmul_mx(
-                out=bank[:],
-                lhsT=wwd[:, t].rearrange("p m b -> p (m b)").bitcast(FP4X4),
-                lhsT_scale=wsd[:, t],
+                out=y_bank[:],
+                lhsT=w_dealt_words[:, t].rearrange("p m b -> p (m b)").bitcast(FP4X4),
+                lhsT_scale=w_dealt_scales[:, t],
                 rhs=xq_words[:].bitcast(FP8X4),
                 rhs_scale=xq_scales[:],
                 start=True,
                 stop=True,
             )
-            nc.scalar.activation(y[t][:, :S], bank[:], ACT.Copy)
+            nc.scalar.activation(y[t][:, :S], y_bank[:], ACT.Copy)
 
-        xb_words, xb_scales = pick_dealt(cb_l, "xb")
-        yg = [held.tile([P, S], F32, name=f"yg{t}") for t in range(PACK)]
+        xb_words, xb_scales = pick_dealt(cb_list, "xb")
+        gy = [held.tile([P, S], F32, name=f"gy{t}") for t in range(PACK)]
         for t in range(PACK):
-            nc.vector.tensor_scalar(yg[t][:], y[t][:, :S], g1[:, t : t + 1], None, ALU.mult)
-        xa_words, xa_scales = pick_dealt(ca_l, "xa")
+            nc.vector.tensor_scalar(gy[t][:], y[t][:, :S], gs_rows[:, t : t + 1], None, ALU.mult)
+        xa_words, xa_scales = pick_dealt(ca_list, "xa")
 
-        def by_fours(ap, order):
-            return ap.rearrange(order + " -> p c t i", i=4)
+        def regroup_views(grouped, sources, run):
+            return [grouped.rearrange("p (c i) t -> p c t i", i=run)] + [
+                source.rearrange("p t (c i) -> p c t i", i=run) for source in sources
+            ]
 
-        def score(grouped, name, words, scales, banks, cols):
-            codes = held.tile([P, cols.stop - cols.start], U32, name=f"{name}_codes", align_bytes=64)
-            plane = held.tile([P, cols.stop - cols.start], U8, name=f"{name}_plane", align_bytes=64)
+        def quantise(grouped, codes, scales):
             nc.vector.quantize_mx(
-                out=codes[:].bitcast(FP8X4), scales=plane[:], in_=grouped[:].rearrange("p c t -> p (c t)")
+                out=codes.bitcast(FP8X4), scales=scales, in_=grouped[:].rearrange("p c t -> p (c t)")
             )
+
+        def score(grouped, name, x_dealt_words, x_dealt_scales, banks, cols):
+            codes = held.tile([P, cols.stop - cols.start], U32, name=f"{name}_codes", align_bytes=64)
+            scales = held.tile([P, cols.stop - cols.start], U8, name=f"{name}_scales", align_bytes=64)
+            quantise(grouped, codes[:], scales[:])
             for t in range(PACK):
                 nc.tensor.matmul_mx(
                     out=banks[t][:, cols],
-                    lhsT=words[:, t].bitcast(FP8X4),
-                    lhsT_scale=scales[:, t],
+                    lhsT=x_dealt_words[:, t].bitcast(FP8X4),
+                    lhsT_scale=x_dealt_scales[:, t],
                     rhs=codes[:].bitcast(FP8X4),
-                    rhs_scale=plane[:],
+                    rhs_scale=scales[:],
                     start=True,
                     stop=True,
                 )
 
-        b_banks = [psum.tile([P, S], F32, name=f"bank_b{t}", tag=f"first{t}") for t in range(PACK)]
+        b_banks = [psum.tile([P, S], F32, name=f"b_bank{t}", tag=f"y_then_b{t}") for t in range(PACK)]
         z2 = held.tile([P, PACK, S], F32, name="z2")
-
-        def extremes(t, cols):
-            mb = ring.tile([P, HALF, MEMBERS], F32, name="mb", tag="picked")
-            for c in range(2):
-                nc.scalar.activation(
-                    mb[:, c * HALF // 2 : (c + 1) * HALF // 2, :].rearrange("p j m -> p (j m)"),
-                    y[t][:].indirect(entries(n3_l, MEMBERS * (cols.start + c * HALF // 2), MEMBERS * HALF // 2)),
-                    ACT.Copy,
-                )
-            lo = ring.tile([P, HALF, 2], F32, name="lo")
-            hi = ring.tile([P, HALF, 2], F32, name="hi")
-            mn = ring.tile([P, HALF], F32, name="mn")
-            mx = late.tile([P, HALF], F32, name="mx")
-            gap = late.tile([P, HALF], F32, name="gap")
-            th = late.tile([P, HALF], F32, name="th")
-            nc.vector.tensor_tensor(lo[:], mb[:, :, 0:2], mb[:, :, 2:4], ALU.min)
-            nc.vector.tensor_tensor(hi[:], mb[:, :, 0:2], mb[:, :, 2:4], ALU.max)
-            nc.vector.tensor_tensor(mn[:], lo[:, :, 0], lo[:, :, 1], ALU.min)
-            nc.vector.tensor_tensor(mx[:], hi[:, :, 0], hi[:, :, 1], ALU.max)
-            nc.vector.tensor_tensor(gap[:], y[t][:, cols], mn[:], ALU.subtract)
-            nc.scalar.activation(th[:], gap[:], ACT.Tanh)
-            return lambda: nc.vector.scalar_tensor_tensor(
-                z2[:, t, cols], mx[:], g2[:, t : t + 1], th[:], ALU.mult, ALU.mult
-            )
-
+        member_tiles = [held.tile([P, MEMBER_RUN], F32, name=f"members{i}") for i in range(MEMBER_BUFFERS)]
+        pair_max_tiles = [held.tile([P, 2 * HALF], F32, name=f"pair_max{i}") for i in range(2)]
         low = held.tile([P, PACK, S], F32, name="low")
         cut = held.tile([P, PACK, S], F32, name="cut")
+        pa0 = held.tile([P, S], F32, name="pa0")
+        pb0 = held.tile([P, S], F32, name="pb0")
+        high_tiles = [held.tile([P, S], F32, name=f"high{i}") for i in range(3)]
 
-        pab0 = held.tile([P, 2, S], F32, name="pab0")
+        third_last_members = member_tiles[(STEPS - 3) % MEMBER_BUFFERS]
+        pa_pb = [
+            (pa0[:], pb0[:]),
+            (third_last_members[:, :S], third_last_members[:, S:]),
+            (pair_max_tiles[(STEPS - 1) % 2][:], pa0[:]),
+            (pb0[:], high_tiles[0][:]),
+        ]
+        pieces = [(which, cols) for which in range(2) for cols in HALVES]
+        waiting = []
 
         def neighbours(t, which, cols):
-            return yg[t][:].indirect(entries((n1_l, n2_l)[which], cols.start, HALF))
+            return gy[t][:].indirect(entries((n1_list, n2_list)[which], cols.start, HALF))
+
+        def z2_step(step):
+            t, cols = step // 2, HALVES[step % 2]
+            members = member_tiles[step % MEMBER_BUFFERS]
+            nc.scalar.activation(
+                members[:], y[t][:].indirect(entries(n3_list, MEMBERS * cols.start, MEMBER_RUN)), ACT.Copy
+            )
+            members = members[:].rearrange("p (j m) -> p j m", m=MEMBERS)
+            pair_min = {PA_STEP: pa0, PB_STEP: pb0}.get(step) or ring.tile([P, 2 * HALF], F32, name="pair_min")
+            pair_min = pair_min[:].rearrange("p (j m) -> p j m", m=2)
+            pair_max = pair_max_tiles[step % 2][:].rearrange("p (j m) -> p j m", m=2)
+            mn = ring.tile([P, HALF], F32, name="mn")
+            mx = late.tile([P, HALF], F32, name="mx")
+            th = late.tile([P, HALF], F32, name="th")
+            gap = late.tile([P, HALF], F32, name="gap")
+            nc.vector.tensor_tensor(pair_min, members[:, :, 0:2], members[:, :, 2:4], ALU.min)
+            nc.vector.tensor_tensor(pair_max, members[:, :, 0:2], members[:, :, 2:4], ALU.max)
+            nc.vector.tensor_tensor(mn[:], pair_min[:, :, 0], pair_min[:, :, 1], ALU.min)
+            if len(waiting) == LAG:
+                waiting.pop(0)()
+            nc.vector.tensor_tensor(gap[:], y[t][:, cols], mn[:], ALU.subtract)
+            nc.vector.tensor_tensor(mx[:], pair_max[:, :, 0], pair_max[:, :, 1], ALU.max)
+            nc.scalar.activation(th[:], gap[:], ACT.Tanh)
+            waiting.append(
+                lambda: nc.vector.scalar_tensor_tensor(
+                    z2[:, t, cols], mx[:], gs2_rows[:, t : t + 1], th[:], ALU.mult, ALU.mult
+                )
+            )
 
         def median_parts(t):
-            high = ring.tile([P, S], F32, name="high")
-            if t == 0:
-                pab = pab0
-            else:
-                pab = ring.tile([P, 2, S], F32, name="pab", tag="picked")
-                for which in range(2):
-                    for cols in HALVES:
-                        nc.scalar.activation(pab[:, which, cols], neighbours(t, which, cols), ACT.Copy)
-            nc.vector.tensor_tensor(high[:], yg[t][:], pab[:, 0, :], ALU.max)
-            nc.vector.tensor_tensor(low[:, t, :], yg[t][:], pab[:, 0, :], ALU.min)
-            nc.vector.tensor_tensor(cut[:, t, :], high[:], pab[:, 1, :], ALU.min)
+            high = high_tiles[0 if t == 0 else 2 - t % 2]
+            pa, pb = pa_pb[t]
+            for which, cols in pieces[VECTOR_PIECES if t == 0 else 0 :]:
+                nc.scalar.activation(pa_pb[t][which][:, cols], neighbours(t, which, cols), ACT.Copy)
+            nc.vector.tensor_tensor(high[:], gy[t][:], pa, ALU.max)
+            nc.vector.tensor_tensor(low[:, t, :], gy[t][:], pa, ALU.min)
+            nc.vector.tensor_tensor(cut[:, t, :], high[:], pb, ALU.min)
 
-        waiting = []
-        for t in range(PACK):
-            for cols in HALVES:
-                waiting.append(extremes(t, cols))
-                if len(waiting) > LAG:
-                    waiting.pop(0)()
-            nc.vector.tensor_copy(pab0[:, t // 2, HALVES[t % 2]], neighbours(0, t // 2, HALVES[t % 2]))
+        for step in range(STEPS):
+            z2_step(step)
+            for which, cols in pieces[:VECTOR_PIECES]:
+                if step == (PA_STEP, PB_STEP)[which]:
+                    nc.vector.tensor_copy(pa_pb[0][which][:, cols], neighbours(0, which, cols))
         median_parts(0)
-        for finish in waiting:
-            finish()
+        for product in waiting:
+            product()
         z2_grouped = held.tile([P, S, PACK], BF16, name="z2_grouped", align_bytes=64)
-        nc.vector.tensor_copy(by_fours(z2_grouped[:], "p (c i) t"), by_fours(z2[:], "p t (c i)"))
+        nc.vector.tensor_copy(*regroup_views(z2_grouped[:], [z2[:]], 4))
         score(z2_grouped, "z2", xb_words, xb_scales, b_banks, slice(0, S))
         for t in range(1, PACK):
             median_parts(t)
 
         b = [held.tile([P, S], F32, name=f"b{t}") for t in range(PACK)]
-        bn = [held.tile([P, S], F32, name=f"bn{t}") for t in range(PACK)]
+        bn_tiles = [held.tile([P, S], F32, name=f"bn{t}") for t in range(PACK - 1)]
+        bn = [(tile[:, :HALF], tile[:, HALF:]) for tile in bn_tiles] + [(low[:, 0, HALF:], low[:, 1, HALF:])]
         for t in range(PACK):
             nc.scalar.activation(b[t][:], b_banks[t][:], ACT.Copy, scale=SCORE_SCALE)
-            for cols in HALVES:
-                nc.scalar.activation(bn[t][:, cols], b[t][:].indirect(entries(n5_l, cols.start, HALF)), ACT.Copy)
+        for t in range(PACK - 1):
+            for h, cols in enumerate(HALVES):
+                nc.scalar.activation(bn[t][h], b[t][:].indirect(entries(n5_list, cols.start, HALF)), ACT.Copy)
 
-        a_banks = [psum.tile([P, S], F32, name=f"bank_a{t}", tag=f"second{t}") for t in range(PACK)]
+        a_banks = [psum.tile([P, S], F32, name=f"a_bank{t}") for t in range(PACK)]
         a = [held.tile([P, S], F32, name=f"a{t}") for t in range(PACK)]
         z_grouped = [held.tile([P, HALF, PACK], BF16, name=f"z_grouped{h}", align_bytes=64) for h in range(2)]
         for h, cols in enumerate(HALVES):
-            nc.vector.tensor_tensor(
-                by_fours(z_grouped[h][:], "p (c i) t"),
-                by_fours(low[:, :, cols], "p t (c i)"),
-                by_fours(cut[:, :, cols], "p t (c i)"),
-                ALU.max,
-            )
-            score(z_grouped[h], f"z_{h}", xa_words, xa_scales, a_banks, cols)
-            for t in range(PACK):
-                nc.scalar.activation(a[t][:, cols], a_banks[t][:, cols], ACT.Copy, scale=SCORE_SCALE)
+            nc.vector.tensor_tensor(*regroup_views(z_grouped[h][:], [low[:, :, cols], cut[:, :, cols]], 2), ALU.max)
+        score(z_grouped[0], "z_first", xa_words, xa_scales, a_banks, HALVES[0])
+        for t in range(PACK):
+            nc.scalar.activation(a[t][:, :HALF], a_banks[t][:, :HALF], ACT.Copy, scale=SCORE_SCALE)
+        score(z_grouped[1], "z_second", xa_words, xa_scales, a_banks, HALVES[1])
+        for h, cols in enumerate(HALVES):
+            nc.vector.tensor_copy(bn[PACK - 1][h], b[PACK - 1][:].indirect(entries(n5_list, cols.start, HALF)))
 
         out_rows = out_0.rearrange("(p t) j -> p t j", t=PACK)
         out_words = out_1[0].rearrange("p c r -> p (c r)").bitcast(I32)
-        out_plane = held.tile([P, S], U8, name="out_plane", align_bytes=64)
-        for h in range(2):
-            cols = slice(h * HALF, (h + 1) * HALF)
+        out_scales = held.tile([P, S], U8, name="out_scales", align_bytes=64)
+        larger = [held.tile([P, S], F32, name=f"larger{t}") for t in range(PACK)]
+        out_grouped = [held.tile([P, HALF, PACK], BF16, name=f"out_grouped{h}", align_bytes=64) for h in range(2)]
+        for h, cols in enumerate(HALVES):
             result = held.tile([P, PACK, HALF], F32, name=f"result{h}")
             for t in range(PACK):
-                an = ring.tile([P, HALF], F32, name="an")
-                larger = ring.tile([P, HALF], F32, name="larger")
-                smaller = ring.tile([P, HALF], F32, name="smaller")
-                nc.scalar.activation(an[:], a[t][:].indirect(entries(n4_l, h * HALF, HALF)), ACT.Copy)
-                nc.vector.tensor_tensor(larger[:], a[t][:, cols], bn[t][:, cols], ALU.max)
+                an = ring.tile([P, HALF], F32, name="an", bufs=PACK)
+                smaller = ring.tile([P, HALF], F32, name="smaller", bufs=PACK - 1)
+                if h == 0:
+                    nc.scalar.activation(a[t][:, HALF:], a_banks[t][:, HALF:], ACT.Copy, scale=SCORE_SCALE)
+                    nc.vector.tensor_tensor(larger[t][:, :HALF], a[t][:, :HALF], bn[t][0], ALU.max)
+                nc.scalar.activation(an[:], a[t][:].indirect(entries(n4_list, cols.start, HALF)), ACT.Copy)
+                if h == 0:
+                    nc.vector.tensor_tensor(larger[t][:, HALF:], a[t][:, HALF:], bn[t][1], ALU.max)
                 nc.vector.tensor_tensor(smaller[:], an[:], b[t][:, cols], ALU.min)
-                nc.vector.tensor_tensor(result[:, t, :], larger[:], smaller[:], ALU.subtract)
+                nc.vector.tensor_tensor(result[:, t, :], larger[t][:, cols], smaller[:], ALU.subtract)
                 nc.sync.dma_start(out_rows[:, t, cols], result[:, t, :])
-            out_grouped = held.tile([P, HALF, PACK], BF16, name=f"out_grouped{h}", align_bytes=64)
+            nc.vector.tensor_copy(*regroup_views(out_grouped[h][:], [result[:]], 4))
+        for h, cols in enumerate(HALVES):
             out_codes = held.tile([P, HALF], U32, name=f"out_codes{h}", align_bytes=64)
-            nc.vector.tensor_copy(by_fours(out_grouped[:], "p (c i) t"), by_fours(result[:], "p t (c i)"))
-            nc.vector.quantize_mx(
-                out=out_codes[:].bitcast(FP8X4),
-                scales=out_plane[:, cols],
-                in_=out_grouped[:].rearrange("p c t -> p (c t)"),
-            )
+            quantise(out_grouped[h], out_codes[:], out_scales[:, cols])
             nc.sync.dma_start(out_words[:, cols], out_codes[:].bitcast(I32))
-        for q in range(4):
-            nc.sync.dma_start(
-                out_2[0, 4 * q : 4 * q + 4, :].bitcast(I32), out_plane[32 * q : 32 * q + 4, :].bitcast(I32)
-            )
+        for q in range(QUADRANTS):
+            sbuf_rows, dram_rows = scale_rows(out_scales, out_2, q)
+            (nc.sync, nc.scalar)[q % 2].dma_start(dram_rows, sbuf_rows)

from contextlib import ExitStack

import concourse.mybir as mybir

F32 = mybir.dt.float32
BF16 = mybir.dt.bfloat16
I32 = mybir.dt.int32
U32 = mybir.dt.uint32
U16 = mybir.dt.uint16
U8 = mybir.dt.uint8
FP8X4 = mybir.dt.float8_e4m3fn_x4
FP4X4 = mybir.dt.float4_e2m1fn_x4
ALU = mybir.AluOpType
ACT = mybir.ActivationFunctionType

P = 128
PACK = 4
QUADRANTS = 4
K, T, S = 512, 2048, 512
MEMBERS = 4
HALF = S // 2
HALVES = (slice(0, HALF), slice(HALF, S))
LIST_COLUMN = 16
MEMBER_RUN = MEMBERS * HALF
Y_WINDOW = MEMBER_RUN + LIST_COLUMN
STEPS = PACK * len(HALVES)
MEMBER_BUFFERS = 3
LAG = MEMBER_BUFFERS
VECTOR_PIECES, PA_STEP, PB_STEP = 3, 1, 4
SCORE_SCALE = 0.0625
FLOPS = 3 * 2 * K * S * S


def tile_picked_twocdmaxbmedgtan_none_po_kernel(
    tc, x_words, x_scales, w1_words, w1_scales, gs, gs2, offs, n1, n2, n3, ca, cb, n4, n5, out_0, out_1, out_2
):
    nc = tc.nc
    with ExitStack() as ctx:
        held = ctx.enter_context(tc.tile_pool(name="held", bufs=1))
        ring = ctx.enter_context(tc.tile_pool(name="ring", bufs=2))
        late = ctx.enter_context(tc.tile_pool(name="late", bufs=LAG + 2))
        psum = ctx.enter_context(tc.psum_pool(name="psum", bufs=1))

        def load_list(src, name):
            offsets = held.tile([P, src.shape[1]], U16, name=name)
            nc.sync.dma_start(offsets[:], src)
            return offsets

        def entries(offsets, first, count):
            return offsets[:, first // LIST_COLUMN : (first + count) // LIST_COLUMN]

        def scale_rows(tile, dram, quadrant):
            return (
                tile[32 * quadrant : 32 * quadrant + 4, :].bitcast(I32),
                dram[0, 4 * quadrant : 4 * quadrant + 4, :].bitcast(I32),
            )

        def load_weights(src, name):
            weights = held.tile([P, PACK], F32, name=name)
            nc.sync.dma_start(weights[:], src.rearrange("(p t) o -> p (t o)", t=PACK))
            return weights

        x_word_table = held.tile([P, T], U32, name="x_word_table")
        x_scale_table = held.tile([P, T], U8, name="x_scale_table")
        w_words = held.tile([P, 2 * S], U8, name="w_words")
        w_scales = held.tile([P, S], U8, name="w_scales")
        nc.vector.memset(x_scale_table[:].bitcast(I32), 0)
        nc.vector.memset(w_scales[:].bitcast(I32), 0)
        offs_list = load_list(offs, "offs_list")
        n3_list = load_list(n3, "n3_list")
        nc.sync.dma_start(w_words[:], w1_words[0])
        for q in range(QUADRANTS):
            nc.sync.dma_start(*scale_rows(x_scale_table, x_scales, q))
        nc.sync.dma_start(x_word_table[:].bitcast(I32), x_words[0].rearrange("p c r -> p (c r)").bitcast(I32))
        for q in range(QUADRANTS):
            nc.sync.dma_start(*scale_rows(w_scales, w1_scales, q))
        gs_rows = load_weights(gs, "gs_rows")
        n1_list = load_list(n1, "n1_list")
        cb_list = load_list(cb, "cb_list")
        ca_list = load_list(ca, "ca_list")
        n2_list = load_list(n2, "n2_list")
        gs2_rows = load_weights(gs2, "gs2_rows")
        n5_list = load_list(n5, "n5_list")
        n4_list = load_list(n4, "n4_list")

        y = [held.tile([P, Y_WINDOW], F32, name=f"y{t}") for t in range(PACK)]
        for t in range(PACK):
            nc.vector.memset(y[t][:, S:], 0.0)

        w_dealt_words = held.tile([P, PACK, P, 2], U8, name="w_dealt_words", align_bytes=64)
        w_dealt_scales = held.tile([P, PACK, P], U8, name="w_dealt_scales", align_bytes=64)
        nc.vector.tensor_copy(w_dealt_words[:], w_words[:].rearrange("p (m t b) -> p t m b", t=PACK, b=2))
        nc.vector.tensor_copy(w_dealt_scales[:], w_scales[:].rearrange("p (m t) -> p t m", t=PACK))

        def pick(offsets, name):
            words = held.tile([P, S], U32, name=f"{name}_words", align_bytes=64)
            scales = held.tile([P, S], U8, name=f"{name}_scales", align_bytes=64)
            nc.vector.tensor_copy(words[:], x_word_table[:].indirect(offsets[:]))
            nc.vector.tensor_copy(scales[:], x_scale_table[:].indirect(offsets[:]))
            return words, scales

        def pick_dealt(offsets, name):
            words, scales = pick(offsets, name)
            dealt_words = held.tile([P, PACK, P], U32, name=f"{name}_dealt_words", align_bytes=64)
            dealt_scales = held.tile([P, PACK, P], U8, name=f"{name}_dealt_scales", align_bytes=64)
            nc.vector.tensor_copy(
                dealt_words[:].bitcast(I32).rearrange("p t m -> p m t"),
                words[:].bitcast(I32).rearrange("p (m t) -> p m t", t=PACK),
            )
            nc.vector.tensor_copy(dealt_scales[:], scales[:].rearrange("p (m t) -> p t m", t=PACK))
            return dealt_words, dealt_scales

        xq_words, xq_scales = pick(offs_list, "xq")
        for t in range(PACK):
            y_bank = psum.tile([P, S], F32, name=f"y_bank{t}", tag=f"y_then_b{t}")
            nc.tensor.matmul_mx(
                out=y_bank[:],
                lhsT=w_dealt_words[:, t].rearrange("p m b -> p (m b)").bitcast(FP4X4),
                lhsT_scale=w_dealt_scales[:, t],
                rhs=xq_words[:].bitcast(FP8X4),
                rhs_scale=xq_scales[:],
                start=True,
                stop=True,
            )
            nc.scalar.activation(y[t][:, :S], y_bank[:], ACT.Copy)

        xb_words, xb_scales = pick_dealt(cb_list, "xb")
        gy = [held.tile([P, S], F32, name=f"gy{t}") for t in range(PACK)]
        for t in range(PACK):
            nc.vector.tensor_scalar(gy[t][:], y[t][:, :S], gs_rows[:, t : t + 1], None, ALU.mult)
        xa_words, xa_scales = pick_dealt(ca_list, "xa")

        def regroup_views(grouped, sources, run):
            return [grouped.rearrange("p (c i) t -> p c t i", i=run)] + [
                source.rearrange("p t (c i) -> p c t i", i=run) for source in sources
            ]

        def quantise(grouped, codes, scales):
            nc.vector.quantize_mx(
                out=codes.bitcast(FP8X4), scales=scales, in_=grouped[:].rearrange("p c t -> p (c t)")
            )

        def score(grouped, name, x_dealt_words, x_dealt_scales, banks, cols):
            codes = held.tile([P, cols.stop - cols.start], U32, name=f"{name}_codes", align_bytes=64)
            scales = held.tile([P, cols.stop - cols.start], U8, name=f"{name}_scales", align_bytes=64)
            quantise(grouped, codes[:], scales[:])
            for t in range(PACK):
                nc.tensor.matmul_mx(
                    out=banks[t][:, cols],
                    lhsT=x_dealt_words[:, t].bitcast(FP8X4),
                    lhsT_scale=x_dealt_scales[:, t],
                    rhs=codes[:].bitcast(FP8X4),
                    rhs_scale=scales[:],
                    start=True,
                    stop=True,
                )

        b_banks = [psum.tile([P, S], F32, name=f"b_bank{t}", tag=f"y_then_b{t}") for t in range(PACK)]
        z2 = held.tile([P, PACK, S], F32, name="z2")
        member_tiles = [held.tile([P, MEMBER_RUN], F32, name=f"members{i}") for i in range(MEMBER_BUFFERS)]
        pair_max_tiles = [held.tile([P, 2 * HALF], F32, name=f"pair_max{i}") for i in range(2)]
        low = held.tile([P, PACK, S], F32, name="low")
        cut = held.tile([P, PACK, S], F32, name="cut")
        pa0 = held.tile([P, S], F32, name="pa0")
        pb0 = held.tile([P, S], F32, name="pb0")
        high_tiles = [held.tile([P, S], F32, name=f"high{i}") for i in range(3)]

        third_last_members = member_tiles[(STEPS - 3) % MEMBER_BUFFERS]
        pa_pb = [
            (pa0[:], pb0[:]),
            (third_last_members[:, :S], third_last_members[:, S:]),
            (pair_max_tiles[(STEPS - 1) % 2][:], pa0[:]),
            (pb0[:], high_tiles[0][:]),
        ]
        pieces = [(which, cols) for which in range(2) for cols in HALVES]
        waiting = []

        def neighbours(t, which, cols):
            return gy[t][:].indirect(entries((n1_list, n2_list)[which], cols.start, HALF))

        def z2_step(step):
            t, cols = step // 2, HALVES[step % 2]
            members = member_tiles[step % MEMBER_BUFFERS]
            nc.scalar.activation(
                members[:], y[t][:].indirect(entries(n3_list, MEMBERS * cols.start, MEMBER_RUN)), ACT.Copy
            )
            members = members[:].rearrange("p (j m) -> p j m", m=MEMBERS)
            pair_min = {PA_STEP: pa0, PB_STEP: pb0}.get(step) or ring.tile([P, 2 * HALF], F32, name="pair_min")
            pair_min = pair_min[:].rearrange("p (j m) -> p j m", m=2)
            pair_max = pair_max_tiles[step % 2][:].rearrange("p (j m) -> p j m", m=2)
            mn = ring.tile([P, HALF], F32, name="mn")
            mx = late.tile([P, HALF], F32, name="mx")
            th = late.tile([P, HALF], F32, name="th")
            gap = late.tile([P, HALF], F32, name="gap")
            nc.vector.tensor_tensor(pair_min, members[:, :, 0:2], members[:, :, 2:4], ALU.min)
            nc.vector.tensor_tensor(pair_max, members[:, :, 0:2], members[:, :, 2:4], ALU.max)
            nc.vector.tensor_tensor(mn[:], pair_min[:, :, 0], pair_min[:, :, 1], ALU.min)
            if len(waiting) == LAG:
                waiting.pop(0)()
            nc.vector.tensor_tensor(gap[:], y[t][:, cols], mn[:], ALU.subtract)
            nc.vector.tensor_tensor(mx[:], pair_max[:, :, 0], pair_max[:, :, 1], ALU.max)
            nc.scalar.activation(th[:], gap[:], ACT.Tanh)
            waiting.append(
                lambda: nc.vector.scalar_tensor_tensor(
                    z2[:, t, cols], mx[:], gs2_rows[:, t : t + 1], th[:], ALU.mult, ALU.mult
                )
            )

        def median_parts(t):
            high = high_tiles[0 if t == 0 else 2 - t % 2]
            pa, pb = pa_pb[t]
            for which, cols in pieces[VECTOR_PIECES if t == 0 else 0 :]:
                nc.scalar.activation(pa_pb[t][which][:, cols], neighbours(t, which, cols), ACT.Copy)
            nc.vector.tensor_tensor(high[:], gy[t][:], pa, ALU.max)
            nc.vector.tensor_tensor(low[:, t, :], gy[t][:], pa, ALU.min)
            nc.vector.tensor_tensor(cut[:, t, :], high[:], pb, ALU.min)

        for step in range(STEPS):
            z2_step(step)
            for which, cols in pieces[:VECTOR_PIECES]:
                if step == (PA_STEP, PB_STEP)[which]:
                    nc.vector.tensor_copy(pa_pb[0][which][:, cols], neighbours(0, which, cols))
        median_parts(0)
        for product in waiting:
            product()
        z2_grouped = held.tile([P, S, PACK], BF16, name="z2_grouped", align_bytes=64)
        nc.vector.tensor_copy(*regroup_views(z2_grouped[:], [z2[:]], 4))
        score(z2_grouped, "z2", xb_words, xb_scales, b_banks, slice(0, S))
        for t in range(1, PACK):
            median_parts(t)

        b = [held.tile([P, S], F32, name=f"b{t}") for t in range(PACK)]
        bn_tiles = [held.tile([P, S], F32, name=f"bn{t}") for t in range(PACK - 1)]
        bn = [(tile[:, :HALF], tile[:, HALF:]) for tile in bn_tiles] + [(low[:, 0, HALF:], low[:, 1, HALF:])]
        for t in range(PACK):
            nc.scalar.activation(b[t][:], b_banks[t][:], ACT.Copy, scale=SCORE_SCALE)
        for t in range(PACK - 1):
            for h, cols in enumerate(HALVES):
                nc.scalar.activation(bn[t][h], b[t][:].indirect(entries(n5_list, cols.start, HALF)), ACT.Copy)

        a_banks = [psum.tile([P, S], F32, name=f"a_bank{t}") for t in range(PACK)]
        a = [held.tile([P, S], F32, name=f"a{t}") for t in range(PACK)]
        z_grouped = [held.tile([P, HALF, PACK], BF16, name=f"z_grouped{h}", align_bytes=64) for h in range(2)]
        for h, cols in enumerate(HALVES):
            nc.vector.tensor_tensor(*regroup_views(z_grouped[h][:], [low[:, :, cols], cut[:, :, cols]], 2), ALU.max)
        score(z_grouped[0], "z_first", xa_words, xa_scales, a_banks, HALVES[0])
        for t in range(PACK):
            nc.scalar.activation(a[t][:, :HALF], a_banks[t][:, :HALF], ACT.Copy, scale=SCORE_SCALE)
        score(z_grouped[1], "z_second", xa_words, xa_scales, a_banks, HALVES[1])
        for h, cols in enumerate(HALVES):
            nc.vector.tensor_copy(bn[PACK - 1][h], b[PACK - 1][:].indirect(entries(n5_list, cols.start, HALF)))

        out_rows = out_0.rearrange("(p t) j -> p t j", t=PACK)
        out_words = out_1[0].rearrange("p c r -> p (c r)").bitcast(I32)
        out_scales = held.tile([P, S], U8, name="out_scales", align_bytes=64)
        larger = [held.tile([P, S], F32, name=f"larger{t}") for t in range(PACK)]
        out_grouped = [held.tile([P, HALF, PACK], BF16, name=f"out_grouped{h}", align_bytes=64) for h in range(2)]
        for h, cols in enumerate(HALVES):
            result = held.tile([P, PACK, HALF], F32, name=f"result{h}")
            for t in range(PACK):
                an = ring.tile([P, HALF], F32, name="an", bufs=PACK)
                smaller = ring.tile([P, HALF], F32, name="smaller", bufs=PACK - 1)
                if h == 0:
                    nc.scalar.activation(a[t][:, HALF:], a_banks[t][:, HALF:], ACT.Copy, scale=SCORE_SCALE)
                    nc.vector.tensor_tensor(larger[t][:, :HALF], a[t][:, :HALF], bn[t][0], ALU.max)
                nc.scalar.activation(an[:], a[t][:].indirect(entries(n4_list, cols.start, HALF)), ACT.Copy)
                if h == 0:
                    nc.vector.tensor_tensor(larger[t][:, HALF:], a[t][:, HALF:], bn[t][1], ALU.max)
                nc.vector.tensor_tensor(smaller[:], an[:], b[t][:, cols], ALU.min)
                nc.vector.tensor_tensor(result[:, t, :], larger[t][:, cols], smaller[:], ALU.subtract)
                nc.sync.dma_start(out_rows[:, t, cols], result[:, t, :])
            nc.vector.tensor_copy(*regroup_views(out_grouped[h][:], [result[:]], 4))
        for h, cols in enumerate(HALVES):
            out_codes = held.tile([P, HALF], U32, name=f"out_codes{h}", align_bytes=64)
            quantise(out_grouped[h], out_codes[:], out_scales[:, cols])
            nc.sync.dma_start(out_words[:, cols], out_codes[:].bitcast(I32))
        for q in range(QUADRANTS):
            sbuf_rows, dram_rows = scale_rows(out_scales, out_2, q)
            (nc.sync, nc.scalar)[q % 2].dma_start(dram_rows, sbuf_rows)
